import numpy as np
import ml_dtypes


def mxq(x, axis, fmt="e4m3"):
    dtype, down = {"e4m3": (ml_dtypes.float8_e4m3fn, 7), "e5m2": (ml_dtypes.float8_e5m2, 14)}[fmt]
    v = np.moveaxis(np.asarray(x, np.float32).astype(ml_dtypes.bfloat16).astype(np.float64), axis, -1)
    blocks = v.reshape(v.shape[:-1] + (-1, 32))
    amax = np.abs(blocks).max(-1, keepdims=True)
    byte = np.maximum(np.where(amax > 0, np.frexp(amax)[1] - 1 + 127, 0) - down, 1)
    scale = np.exp2(byte - 127.0)
    codes = (blocks / scale).astype(np.float32).astype(dtype).astype(np.float64)
    return np.moveaxis((codes * scale).reshape(v.shape), -1, axis)


WIDE = False


def mx_kscale(k):
    if not WIDE:
        return np.ones(k)
    levels = np.array([10, -10, 5, -5, 0])
    if k % 512:
        return np.exp2(np.random.permutation(np.resize(levels, k // 32))).repeat(32)
    a = np.empty((k // 512, 16))
    for p in range(k // 512):
        a[p, :8] = np.random.permutation(np.resize(levels, 8))
        for g in range(8):
            far = levels[np.abs(levels - a[p, g]) >= 10]
            a[p, g + 8] = far[np.random.randint(len(far))]
    return np.exp2(a.ravel()).repeat(32)


def f64(x):
    return np.asarray(x).astype(np.float64)


def striped(idx):
    return np.tile(idx.reshape(-1, 16).T, (8, 1)).astype(np.uint16)


def unstriped(offs):
    return offs[:16].T.reshape(-1).astype(np.int64)


E2M1 = np.array([0.0, 0.5, 1.0, 1.5, 2.0, 3.0, 4.0, 6.0, -0.0, -0.5, -1.0, -1.5, -2.0, -3.0, -4.0, -6.0])


def pack_weight(w, fmt):
    k, n = w.shape
    w = f64(np.asarray(w, np.float32).astype(ml_dtypes.bfloat16)).reshape(k // 32, 32, n)
    amax = np.abs(w).max(1)
    if fmt == "e4m3":
        byte = np.frexp(amax)[1] - 1 + 127 - 7
    else:
        mant, ex = np.frexp(amax / 6.0)
        byte = np.where(mant > 0.5, ex, ex - 1) + 127
    byte = np.clip(np.where(amax > 0, byte, 1), 1, 254)
    scaled = (w * np.exp2(127.0 - byte)[:, None, :]).reshape(k, n).astype(np.float32)
    by_word = np.ascontiguousarray(scaled.reshape(k // 512, 128, 4, n).transpose(0, 1, 3, 2))
    if fmt == "e4m3":
        words = by_word.astype(ml_dtypes.float8_e4m3fn).view(np.uint8)
    else:
        c = by_word.astype(ml_dtypes.float4_e2m1fn).view(np.uint8) & 0xF
        words = (c[..., 0::2] | (c[..., 1::2] << 4)).reshape(k // 512, 128, 2 * n)
    return np.ascontiguousarray(words), np.ascontiguousarray(byte.astype(np.uint8).reshape(k // 512, 16, n))


def unpack_weight(words, scales, fmt):
    g, _, n = scales.shape
    words = np.ascontiguousarray(words).reshape(g, 128, n, -1)
    if fmt == "e4m3":
        vals = words.view(ml_dtypes.float8_e4m3fn).astype(np.float64)
    else:
        nib = np.empty((g, 128, n, 4), np.uint8)
        nib[..., 0::2] = words & 0xF
        nib[..., 1::2] = words >> 4
        vals = E2M1[nib]
    vals = vals * np.repeat(np.exp2(scales.astype(np.float64) - 127.0), 8, axis=1)[..., None]
    return vals.transpose(0, 1, 3, 2).reshape(g * 512, n)


def pack_table(v):
    words, scales = pack_weight(v, "e4m3")
    return np.concatenate([words.reshape(words.shape[0], -1), scales.reshape(scales.shape[0], -1)], axis=1)


def unpack_table(tab):
    g, t = tab.shape[0], tab.shape[1] // 528
    return unpack_weight(tab[:, :512 * t].reshape(g, 128, t, 4), tab[:, 512 * t:].reshape(g, 16, t), "e4m3")


def split(x):
    m, e = np.frexp(f64(x))
    hi = np.ldexp(np.trunc(16.0 * m) / 16.0, e)
    return hi, f64(x) - hi


def gelu(v):
    return 0.5 * v * (1.0 + np.tanh(np.sqrt(2.0 / np.pi) * (v + 0.044715 * v**3)))


K, M, T, S = 2048, 1024, 512, 256


def setup_inputs():
    n = np.random.standard_normal
    s = mx_kscale(K)[:, None]
    return {
        "tab": pack_table(n((K, T)) * s),
        "w": (n((K, M)) / np.sqrt(K) / s).astype(np.float32),
        "b": (0.3 * n(1024)).astype(np.float32),
        "offs": striped(np.random.permutation(T)[:S]),
    }


def reference(tab, w, b, offs):
    tab_ = unpack_table(tab)[:, unstriped(offs)]
    w_hi, w_lo = split(w)
    w_hi_, w_lo_ = mxq(w_hi, 0, "e4m3"), mxq(w_lo, 0, "e4m3")
    y = w_hi_.T @ tab_ + w_lo_.T @ tab_
    return gelu(y + f64(b)[:, None])

@@ -1,0 +1,191 @@
+from contextlib import ExitStack
+
+import concourse.mybir as mybir
+
+K, M, T, S = 2048, 1024, 512, 256
+FLOPS = 2 * 2 * K * M * S
+
+F32 = mybir.dt.float32
+BF16 = mybir.dt.bfloat16
+I32 = mybir.dt.int32
+U32 = mybir.dt.uint32
+U16 = mybir.dt.uint16
+U8 = mybir.dt.uint8
+FP8X4 = mybir.dt.float8_e4m3fn_x4
+ALU = mybir.AluOpType
+ACT = mybir.ActivationFunctionType
+
+P = 128
+PACK = 4
+K_PASS = P * PACK
+PASSES = K // K_PASS
+M_TILE = 128
+HI, LO = 0, 1
+WIDEST_QUANTIZE = 4096
+
+HI_MASK = 0xFFF0FFF0 - (1 << 32)
+
+CHUNKS = [
+    (0, 0, 128, 64), (0, 128, 128, 128), (0, 256, 256, 256), (0, 512, 512, 512),
+    (1, 0, 1024, 1024),
+    (2, 0, 1024, 1024),
+    (3, 0, 512, 512), (3, 512, 256, 256), (3, 768, 128, 128), (3, 896, 128, 128),
+]
+
+
+def tile_list_tabw_hl_gelu_kernel(tc, tab, w, b, offs, out):
+    nc = tc.nc
+    with ExitStack() as ctx:
+        held = ctx.enter_context(tc.tile_pool(name="held", bufs=1))
+        psum = ctx.enter_context(tc.psum_pool(name="psum", bufs=1))
+
+        offsets = held.tile([P, S // 16], U16, name="offsets")
+        nc.sync.dma_start(offsets[:], offs)
+
+        tab_scales = held.tile([P, T], U8, name="tab_scales", align_bytes=64)
+        nc.gpsimd.memset(tab_scales[:].bitcast(I32), 0)
+
+        warm = held.tile([P, 8], F32, name="warm")
+        nc.gpsimd.memset(warm[:], 0.0)
+        nc.scalar.activation(out=warm[:, 0:1], in_=warm[:, 4:5], func=ACT.Gelu_apprx_tanh)
+
+        tab_words = [held.tile([P, T], U32, name="tab_words%d" % a, align_bytes=64) for a in range(PASSES)]
+        got_words = [held.tile([P, S], U32, name="got_words%d" % a, align_bytes=64) for a in range(PASSES)]
+        got_scales = held.tile([P, S], U8, name="got_scales", align_bytes=64)
+        bias = held.tile([P, M // M_TILE], F32, name="bias")
+
+        n_words = P * T * PACK
+        scale_rows = tab[:, n_words:].rearrange("a (q t) -> a q t", t=T)
+
+        def load_table(a):
+            words = tab[a, 0:n_words].rearrange("(p x) -> p x", p=P).bitcast(I32)
+            nc.sync.dma_start(tab_words[a][:].bitcast(I32), words)
+
+        def load_scales():
+            for q in range(4):
+                nc.sync.dma_start(
+                    tab_scales[32 * q : 32 * q + 16, :].bitcast(I32),
+                    scale_rows[:, 4 * q : 4 * q + 4, :].bitcast(I32),
+                )
+
+        w_view = w.rearrange("(a p t) n -> a p t n", p=P, t=PACK)
+        raw, values, codes, scales = [], [], [], []
+        for i, (a, c0, n, step) in enumerate(CHUNKS):
+            raw.append([held.tile([P, PACK, step], F32, name="raw%d_%d" % (i, s), align_bytes=64) for s in range(n // step)])
+            values.append(held.tile([P, 2, n, PACK], BF16, name="values%d" % i, align_bytes=64))
+            codes.append(held.tile([P, 2, n], U32, name="codes%d" % i, align_bytes=64))
+            scales.append(held.tile([P, 2, n], U8, name="scales%d" % i, align_bytes=64))
+
+        def load_w(i, s=0):
+            a, c0, n, step = CHUNKS[i]
+            nc.sync.dma_start(raw[i][s][:], w_view[a, :, :, c0 + s * step : c0 + (s + 1) * step])
+
+        load_w(0, 0)
+        load_scales()
+        load_w(0, 1)
+        load_table(0)
+        load_w(1)
+        load_w(2)
+        load_table(1)
+        load_w(3)
+        load_table(2)
+        load_w(4)
+        load_table(3)
+        nc.sync.dma_start(bias[:], b.rearrange("(m p) -> p m", p=P), allow_slow_non_contiguous=True)
+        for i in range(5, len(CHUNKS)):
+            load_w(i)
+
+        acc = [psum.tile([P, S], F32, name="acc%d" % m) for m in range(M // M_TILE)]
+        result = [held.tile([P, S], F32, name="result%d" % m) for m in range(M // M_TILE)]
+
+        def gather_words(a):
+            nc.vector.tensor_copy(got_words[a][:], tab_words[a][:].indirect(offsets[:]))
+
+        def gather_scales():
+            nc.vector.tensor_copy(got_scales[:], tab_scales[:].indirect(offsets[:]))
+
+        def piece(i, s, part):
+            step = CHUNKS[i][3]
+            return values[i][:, part, s * step : (s + 1) * step, :]
+
+        def interleave(i):
+            for s in range(len(raw[i])):
+                halves = raw[i][s][:].rearrange("p t n -> p (t n)").bitcast(BF16)
+                upper = halves.rearrange("p (t c i h) -> p c t i h", t=PACK, i=4, h=2)[:, :, :, :, 1]
+                nc.scalar.copy(piece(i, s, HI).rearrange("p (c i) t -> p c t i", i=4), upper)
+
+        def mask(i, s):
+            words = piece(i, s, HI).rearrange("p n t -> p (n t)").bitcast(I32)
+            nc.vector.tensor_scalar(out=words, in0=words, scalar1=HI_MASK, scalar2=None, op0=ALU.bitwise_and)
+
+        def subtract(i, s):
+            nc.vector.tensor_tensor(
+                out=piece(i, s, LO).rearrange("p (c i) t -> p c t i", i=4),
+                in0=raw[i][s][:].rearrange("p t (c i) -> p c t i", i=4),
+                in1=piece(i, s, HI).rearrange("p (c i) t -> p c t i", i=4),
+                op=ALU.subtract,
+            )
+
+        def quantize(i, part0, parts):
+            span = slice(part0, part0 + parts)
+            nc.vector.quantize_mx(
+                out=codes[i][:, span, :].rearrange("p h n -> p (h n)").bitcast(FP8X4),
+                scales=scales[i][:, span, :].rearrange("p h n -> p (h n)"),
+                in_=values[i][:, span, :, :].rearrange("p h n t -> p (h n t)"),
+            )
+
+        def joint(i):
+            return 2 * PACK * CHUNKS[i][2] <= WIDEST_QUANTIZE
+
+        def multiply(i):
+            a, c0, n, step = CHUNKS[i]
+            for part in (HI, LO):
+                for j in range(n // M_TILE):
+                    cols = slice(j * M_TILE, (j + 1) * M_TILE)
+                    nc.tensor.matmul_mx(
+                        out=acc[c0 // M_TILE + j][:],
+                        lhsT=codes[i][:, part, cols].bitcast(FP8X4),
+                        lhsT_scale=scales[i][:, part, cols],
+                        rhs=got_words[a][:].bitcast(FP8X4),
+                        rhs_scale=got_scales[4 * a : P, :],
+                        start=a == 0 and part == HI,
+                        stop=a == PASSES - 1 and part == LO,
+                    )
+
+        def finish(i):
+            a, c0, n, step = CHUNKS[i]
+            for m in range(c0 // M_TILE, (c0 + n) // M_TILE):
+                nc.scalar.activation(
+                    out=result[m][:], in_=acc[m][:], func=ACT.Gelu_apprx_tanh, bias=bias[:, m : m + 1]
+                )
+                nc.sync.dma_start(out[m * M_TILE : (m + 1) * M_TILE, :], result[m][:])
+
+        def end_chunk(i):
+            if joint(i):
+                quantize(i, HI, 2)
+            else:
+                quantize(i, LO, 1)
+            multiply(i)
+            if CHUNKS[i][0] == PASSES - 1:
+                finish(i)
+
+        interleave(0)
+        for i in range(len(CHUNKS)):
+            mask(i, 0)
+            if i == 0:
+                gather_scales()
+            if i == 1:
+                gather_words(0)
+            if i > 0:
+                end_chunk(i - 1)
+            if i in (3, 4, 5):
+                gather_words(i - 2)
+            if not joint(i):
+                quantize(i, HI, 1)
+            if i + 1 < len(CHUNKS):
+                interleave(i + 1)
+            subtract(i, 0)
+            for s in range(1, len(raw[i])):
+                mask(i, s)
+                subtract(i, s)
+        end_chunk(len(CHUNKS) - 1)

@@ -21,14 +21,13 @@ K_PASS = P * PACK
 PASSES = K // K_PASS
 M_TILE = 128
 HI, LO = 0, 1
-WIDEST_QUANTIZE = 4096
 
 HI_MASK = 0xFFF0FFF0 - (1 << 32)
 
 CHUNKS = [
-    (0, 0, 128, 64), (0, 128, 128, 128), (0, 256, 256, 256), (0, 512, 512, 512),
-    (1, 0, 1024, 1024),
-    (2, 0, 1024, 1024),
+    (0, 0, 128, 64), (0, 128, 128, 128), (0, 256, 256, 256), (0, 512, 256, 256), (0, 768, 256, 256),
+    (1, 0, 512, 512), (1, 512, 512, 512),
+    (2, 0, 512, 512), (2, 512, 512, 512),
     (3, 0, 512, 512), (3, 512, 256, 256), (3, 768, 128, 128), (3, 896, 128, 128),
 ]
 
@@ -80,20 +79,23 @@ def tile_list_tabw_hl_gelu_kernel(tc, tab, w, b, offs, out):
             a, c0, n, step = CHUNKS[i]
             nc.sync.dma_start(raw[i][s][:], w_view[a, :, :, c0 + s * step : c0 + (s + 1) * step])
 
-        load_w(0, 0)
-        load_scales()
-        load_w(0, 1)
         load_table(0)
+        load_scales()
+        load_w(0, 0)
+        load_w(0, 1)
         load_w(1)
         load_w(2)
         load_table(1)
         load_w(3)
-        load_table(2)
         load_w(4)
+        load_w(5)
+        load_table(2)
+        load_w(6)
+        load_w(7)
         load_table(3)
-        nc.sync.dma_start(bias[:], b.rearrange("(m p) -> p m", p=P), allow_slow_non_contiguous=True)
-        for i in range(5, len(CHUNKS)):
+        for i in range(8, len(CHUNKS)):
             load_w(i)
+        nc.sync.dma_start(bias[:], b.rearrange("(m p) -> p m", p=P), allow_slow_non_contiguous=True)
 
         acc = [psum.tile([P, S], F32, name="acc%d" % m) for m in range(M // M_TILE)]
         result = [held.tile([P, S], F32, name="result%d" % m) for m in range(M // M_TILE)]
@@ -135,7 +137,7 @@ def tile_list_tabw_hl_gelu_kernel(tc, tab, w, b, offs, out):
             )
 
         def joint(i):
-            return 2 * PACK * CHUNKS[i][2] <= WIDEST_QUANTIZE
+            return i < len(CHUNKS) - 1
 
         def multiply(i):
             a, c0, n, step = CHUNKS[i]
@@ -169,17 +171,15 @@ def tile_list_tabw_hl_gelu_kernel(tc, tab, w, b, offs, out):
             if CHUNKS[i][0] == PASSES - 1:
                 finish(i)
 
+        gather_words(0)
+        gather_scales()
         interleave(0)
         for i in range(len(CHUNKS)):
             mask(i, 0)
-            if i == 0:
-                gather_scales()
-            if i == 1:
-                gather_words(0)
             if i > 0:
                 end_chunk(i - 1)
-            if i in (3, 4, 5):
-                gather_words(i - 2)
+            if i in (2, 5, 7):
+                gather_words({2: 1, 5: 2, 7: 3}[i])
             if not joint(i):
                 quantize(i, HI, 1)
             if i + 1 < len(CHUNKS):

from contextlib import ExitStack

import concourse.mybir as mybir

K, M, T, S = 2048, 1024, 512, 256
FLOPS = 2 * 2 * K * M * S

F32 = mybir.dt.float32
BF16 = mybir.dt.bfloat16
I32 = mybir.dt.int32
U32 = mybir.dt.uint32
U16 = mybir.dt.uint16
U8 = mybir.dt.uint8
FP8X4 = mybir.dt.float8_e4m3fn_x4
ALU = mybir.AluOpType
ACT = mybir.ActivationFunctionType

P = 128
PACK = 4
K_PASS = P * PACK
PASSES = K // K_PASS
M_TILE = 128
HI, LO = 0, 1

HI_MASK = 0xFFF0FFF0 - (1 << 32)

CHUNKS = [
    (0, 0, 128, 64), (0, 128, 128, 128), (0, 256, 256, 256), (0, 512, 256, 256), (0, 768, 256, 256),
    (1, 0, 512, 512), (1, 512, 512, 512),
    (2, 0, 512, 512), (2, 512, 512, 512),
    (3, 0, 512, 512), (3, 512, 256, 256), (3, 768, 128, 128), (3, 896, 128, 128),
]


def tile_list_tabw_hl_gelu_kernel(tc, tab, w, b, offs, out):
    nc = tc.nc
    with ExitStack() as ctx:
        held = ctx.enter_context(tc.tile_pool(name="held", bufs=1))
        psum = ctx.enter_context(tc.psum_pool(name="psum", bufs=1))

        offsets = held.tile([P, S // 16], U16, name="offsets")
        nc.sync.dma_start(offsets[:], offs)

        tab_scales = held.tile([P, T], U8, name="tab_scales", align_bytes=64)
        nc.gpsimd.memset(tab_scales[:].bitcast(I32), 0)

        warm = held.tile([P, 8], F32, name="warm")
        nc.gpsimd.memset(warm[:], 0.0)
        nc.scalar.activation(out=warm[:, 0:1], in_=warm[:, 4:5], func=ACT.Gelu_apprx_tanh)

        tab_words = [held.tile([P, T], U32, name="tab_words%d" % a, align_bytes=64) for a in range(PASSES)]
        got_words = [held.tile([P, S], U32, name="got_words%d" % a, align_bytes=64) for a in range(PASSES)]
        got_scales = held.tile([P, S], U8, name="got_scales", align_bytes=64)
        bias = held.tile([P, M // M_TILE], F32, name="bias")

        n_words = P * T * PACK
        scale_rows = tab[:, n_words:].rearrange("a (q t) -> a q t", t=T)

        def load_table(a):
            words = tab[a, 0:n_words].rearrange("(p x) -> p x", p=P).bitcast(I32)
            nc.sync.dma_start(tab_words[a][:].bitcast(I32), words)

        def load_scales():
            for q in range(4):
                nc.sync.dma_start(
                    tab_scales[32 * q : 32 * q + 16, :].bitcast(I32),
                    scale_rows[:, 4 * q : 4 * q + 4, :].bitcast(I32),
                )

        w_view = w.rearrange("(a p t) n -> a p t n", p=P, t=PACK)
        raw, values, codes, scales = [], [], [], []
        for i, (a, c0, n, step) in enumerate(CHUNKS):
            raw.append([held.tile([P, PACK, step], F32, name="raw%d_%d" % (i, s), align_bytes=64) for s in range(n // step)])
            values.append(held.tile([P, 2, n, PACK], BF16, name="values%d" % i, align_bytes=64))
            codes.append(held.tile([P, 2, n], U32, name="codes%d" % i, align_bytes=64))
            scales.append(held.tile([P, 2, n], U8, name="scales%d" % i, align_bytes=64))

        def load_w(i, s=0):
            a, c0, n, step = CHUNKS[i]
            nc.sync.dma_start(raw[i][s][:], w_view[a, :, :, c0 + s * step : c0 + (s + 1) * step])

        load_table(0)
        load_scales()
        load_w(0, 0)
        load_w(0, 1)
        load_w(1)
        load_w(2)
        load_table(1)
        load_w(3)
        load_w(4)
        load_w(5)
        load_table(2)
        load_w(6)
        load_w(7)
        load_table(3)
        for i in range(8, len(CHUNKS)):
            load_w(i)
        nc.sync.dma_start(bias[:], b.rearrange("(m p) -> p m", p=P), allow_slow_non_contiguous=True)

        acc = [psum.tile([P, S], F32, name="acc%d" % m) for m in range(M // M_TILE)]
        result = [held.tile([P, S], F32, name="result%d" % m) for m in range(M // M_TILE)]

        def gather_words(a):
            nc.vector.tensor_copy(got_words[a][:], tab_words[a][:].indirect(offsets[:]))

        def gather_scales():
            nc.vector.tensor_copy(got_scales[:], tab_scales[:].indirect(offsets[:]))

        def piece(i, s, part):
            step = CHUNKS[i][3]
            return values[i][:, part, s * step : (s + 1) * step, :]

        def interleave(i):
            for s in range(len(raw[i])):
                halves = raw[i][s][:].rearrange("p t n -> p (t n)").bitcast(BF16)
                upper = halves.rearrange("p (t c i h) -> p c t i h", t=PACK, i=4, h=2)[:, :, :, :, 1]
                nc.scalar.copy(piece(i, s, HI).rearrange("p (c i) t -> p c t i", i=4), upper)

        def mask(i, s):
            words = piece(i, s, HI).rearrange("p n t -> p (n t)").bitcast(I32)
            nc.vector.tensor_scalar(out=words, in0=words, scalar1=HI_MASK, scalar2=None, op0=ALU.bitwise_and)

        def subtract(i, s):
            nc.vector.tensor_tensor(
                out=piece(i, s, LO).rearrange("p (c i) t -> p c t i", i=4),
                in0=raw[i][s][:].rearrange("p t (c i) -> p c t i", i=4),
                in1=piece(i, s, HI).rearrange("p (c i) t -> p c t i", i=4),
                op=ALU.subtract,
            )

        def quantize(i, part0, parts):
            span = slice(part0, part0 + parts)
            nc.vector.quantize_mx(
                out=codes[i][:, span, :].rearrange("p h n -> p (h n)").bitcast(FP8X4),
                scales=scales[i][:, span, :].rearrange("p h n -> p (h n)"),
                in_=values[i][:, span, :, :].rearrange("p h n t -> p (h n t)"),
            )

        def joint(i):
            return i < len(CHUNKS) - 1

        def multiply(i):
            a, c0, n, step = CHUNKS[i]
            for part in (HI, LO):
                for j in range(n // M_TILE):
                    cols = slice(j * M_TILE, (j + 1) * M_TILE)
                    nc.tensor.matmul_mx(
                        out=acc[c0 // M_TILE + j][:],
                        lhsT=codes[i][:, part, cols].bitcast(FP8X4),
                        lhsT_scale=scales[i][:, part, cols],
                        rhs=got_words[a][:].bitcast(FP8X4),
                        rhs_scale=got_scales[4 * a : P, :],
                        start=a == 0 and part == HI,
                        stop=a == PASSES - 1 and part == LO,
                    )

        def finish(i):
            a, c0, n, step = CHUNKS[i]
            for m in range(c0 // M_TILE, (c0 + n) // M_TILE):
                nc.scalar.activation(
                    out=result[m][:], in_=acc[m][:], func=ACT.Gelu_apprx_tanh, bias=bias[:, m : m + 1]
                )
                nc.sync.dma_start(out[m * M_TILE : (m + 1) * M_TILE, :], result[m][:])

        def end_chunk(i):
            if joint(i):
                quantize(i, HI, 2)
            else:
                quantize(i, LO, 1)
            multiply(i)
            if CHUNKS[i][0] == PASSES - 1:
                finish(i)

        gather_words(0)
        gather_scales()
        interleave(0)
        for i in range(len(CHUNKS)):
            mask(i, 0)
            if i > 0:
                end_chunk(i - 1)
            if i in (2, 5, 7):
                gather_words({2: 1, 5: 2, 7: 3}[i])
            if not joint(i):
                quantize(i, HI, 1)
            if i + 1 < len(CHUNKS):
                interleave(i + 1)
            subtract(i, 0)
            for s in range(1, len(raw[i])):
                mask(i, s)
                subtract(i, s)
        end_chunk(len(CHUNKS) - 1)
